import numpy as np
import ml_dtypes


def mxq(x, axis, fmt="e4m3"):
    dtype, down = {"e4m3": (ml_dtypes.float8_e4m3fn, 7), "e5m2": (ml_dtypes.float8_e5m2, 14)}[fmt]
    v = np.moveaxis(np.asarray(x, np.float32).astype(ml_dtypes.bfloat16).astype(np.float64), axis, -1)
    blocks = v.reshape(v.shape[:-1] + (-1, 32))
    amax = np.abs(blocks).max(-1, keepdims=True)
    byte = np.maximum(np.where(amax > 0, np.frexp(amax)[1] - 1 + 127, 0) - down, 1)
    scale = np.exp2(byte - 127.0)
    codes = (blocks / scale).astype(np.float32).astype(dtype).astype(np.float64)
    return np.moveaxis((codes * scale).reshape(v.shape), -1, axis)


WIDE = False


def mx_kscale(k):
    if not WIDE:
        return np.ones(k)
    levels = np.array([10, -10, 5, -5, 0])
    if k % 512:
        return np.exp2(np.random.permutation(np.resize(levels, k // 32))).repeat(32)
    a = np.empty((k // 512, 16))
    for p in range(k // 512):
        a[p, :8] = np.random.permutation(np.resize(levels, 8))
        for g in range(8):
            far = levels[np.abs(levels - a[p, g]) >= 10]
            a[p, g + 8] = far[np.random.randint(len(far))]
    return np.exp2(a.ravel()).repeat(32)


def f64(x):
    return np.asarray(x).astype(np.float64)


def striped(idx):
    return np.tile(idx.reshape(-1, 16).T, (8, 1)).astype(np.uint16)


def unstriped(offs):
    return offs[:16].T.reshape(-1).astype(np.int64)


def striped8(idx):
    return np.concatenate([x.reshape(-1, 16).T for x in idx]).astype(np.uint16)


def runs(offs, k):
    lists = np.stack([offs[16 * r : 16 * r + 16].T.reshape(-1) for r in range(8)]).astype(np.int64)
    return lists[np.arange(k) % 512 // 64]


def pack_weight(w):
    k, n = w.shape
    w = f64(np.asarray(w, np.float32).astype(ml_dtypes.bfloat16)).reshape(k // 32, 32, n)
    amax = np.abs(w).max(1)
    byte = np.clip(np.where(amax > 0, np.frexp(amax)[1] - 1 + 127 - 7, 1), 1, 254)
    scaled = (w * np.exp2(127.0 - byte)[:, None, :]).reshape(k, n).astype(np.float32)
    words = np.ascontiguousarray(scaled.reshape(k // 512, 128, 4, n).transpose(0, 1, 3, 2)).astype(ml_dtypes.float8_e4m3fn).view(np.uint8)
    return words, np.ascontiguousarray(byte.astype(np.uint8).reshape(k // 512, 16, n))


def unpack_weight(words, scales):
    g, p, n, _ = words.shape
    vals = np.ascontiguousarray(words).view(ml_dtypes.float8_e4m3fn).astype(np.float64) * np.repeat(np.exp2(scales.astype(np.float64) - 127.0), 8, axis=1)[..., None]
    return vals.transpose(0, 1, 3, 2).reshape(g * 512, n)


K, T, S, N, G, H, U = 512, 2048, 512, 512, 2048, 512, 1024


def setup_inputs():
    n = np.random.standard_normal
    s = mx_kscale(K)[:, None]
    u = mx_kscale(S)
    packed_xT = pack_weight(n((K, T)) * s)
    packed_dT = pack_weight(n((K, G)) / s)
    return {
        "x_words": packed_xT[0],
        "x_scales": packed_xT[1],
        "d_words": packed_dT[0],
        "d_scales": packed_dT[1],
        "gn": (np.random.uniform(0.5, 1.5, (H, 1)) * u[:, None]).astype(np.float32),
        "w1": (n((H, N)) / np.sqrt(H) / u[:, None]).astype(np.float32),
        "mem": n((N, U)).astype(np.float32),
        "offs": striped(np.random.permutation(T)[:S]),
        "k1": striped8(np.random.randint(0, G, (8, H))),
        "n1": striped8(np.stack([np.random.permutation(S) for _ in range(8)])),
        "n2": striped8(np.stack([np.random.permutation(S) for _ in range(8)])),
        "n3": striped8(np.stack([np.random.permutation(S) for _ in range(8)])),
        "n4": striped(np.random.permutation(U)[:S]),
    }


def reference(x_words, x_scales, d_words, d_scales, gn, w1, mem, offs, k1, n1, n2, n3, n4):
    d_k1 = unpack_weight(d_words, d_scales)[np.arange(K)[:, None], runs(k1, K)]
    xq = unpack_weight(x_words, x_scales)[:, unstriped(offs)]
    h = 0.0625 * (d_k1.T @ xq)
    z = f64(gn) * (h + h[np.arange(H)[:, None], runs(n1, H)] - (np.maximum(h[np.arange(H)[:, None], runs(n2, H)], h[np.arange(H)[:, None], runs(n3, H)])))
    h2 = mxq(f64(w1), 0, "e4m3").T @ mxq(z, 0, "e4m3")
    out = f64(mem).copy()
    out[:, unstriped(n4)] = h2
    return out

@@ -1,0 +1,182 @@
+from contextlib import ExitStack
+
+import concourse.mybir as mybir
+
+K, T, S, N, G, H, U = 512, 2048, 512, 512, 2048, 512, 1024
+FLOPS = 2 * K * H * S + 2 * H * N * S
+
+F32 = mybir.dt.float32
+BF16 = mybir.dt.bfloat16
+I32 = mybir.dt.int32
+U32 = mybir.dt.uint32
+U16 = mybir.dt.uint16
+U8 = mybir.dt.uint8
+FP8X4 = mybir.dt.float8_e4m3fn_x4
+ALU = mybir.AluOpType
+ACT = mybir.ActivationFunctionType
+
+P = 128
+PACK = 4
+HALF = S // 2
+LINE = 4
+
+
+def tile_picked_pqlaytrimpage_none_p_kernel(tc, x_words, x_scales, d_words, d_scales, gn, w1, mem, offs, k1, n1, n2, n3, n4, out):
+    nc = tc.nc
+    with ExitStack() as ctx:
+        keep = ctx.enter_context(tc.tile_pool(name="keep", bufs=1))
+        big = ctx.enter_context(tc.tile_pool(name="big", bufs=1))
+        work = ctx.enter_context(tc.tile_pool(name="work", bufs=4))
+        psum = ctx.enter_context(tc.psum_pool(name="psum", bufs=8))
+
+        def load_list(src, name):
+            t = keep.tile([P, S // 16], U16, name=name)
+            nc.sync.dma_start(t[:], src)
+            return t
+
+        ds_tab = big.tile([P, G], U8, name="ds_tab", align_bytes=64)
+        xs_tab = big.tile([P, T], U8, name="xs_tab", align_bytes=64)
+        nc.vector.memset(ds_tab[:].bitcast(I32), 0)
+        nc.gpsimd.memset(xs_tab[:].bitcast(I32), 0)
+        nc.sync.dma_start(ds_tab[0:P:8, :].bitcast(I32), d_scales[0].bitcast(I32))
+        nc.sync.dma_start(xs_tab[0:P:8, :].bitcast(I32), x_scales[0].bitcast(I32))
+        k1_sb = load_list(k1, "k1_sb")
+        offs_sb = load_list(offs, "offs_sb")
+        n2_sb = load_list(n2, "n2_sb")
+        dw_tab = big.tile([P, G], I32, name="dw_tab", align_bytes=64)
+        nc.sync.dma_start(dw_tab[:], d_words[0].rearrange("p n t -> p (n t)").bitcast(I32))
+        n3_sb = load_list(n3, "n3_sb")
+        n1_sb = load_list(n1, "n1_sb")
+        n4_sb = load_list(n4, "n4_sb")
+        xw_tab = big.tile([P, T], I32, name="xw_tab", tag="slot_d", align_bytes=64)
+        nc.sync.dma_start(xw_tab[:], x_words[0].rearrange("p n t -> p (n t)").bitcast(I32))
+        gain = keep.tile([P, PACK], F32, name="gain")
+        nc.gpsimd.dma_start(gain[:], gn.rearrange("(p t) o -> p (t o)", t=PACK))
+
+        gabs = keep.tile([P, PACK], F32, name="gabs")
+        nc.scalar.activation(gabs[:], gain[:], ACT.Abs, scale=0.0625)
+        nonneg = keep.tile([P, PACK], F32, name="nonneg")
+        nc.gpsimd.tensor_scalar(nonneg[:], gain[:], 0.0, 2.0, ALU.is_ge, ALU.mult)
+        sign = keep.tile([P, PACK], F32, name="sign")
+        nc.gpsimd.tensor_scalar(sign[:], nonneg[:], 1.0, -1.0, ALU.mult, ALU.add)
+
+        def scale_rows_home(picked, name):
+            plane = big.tile([P, S], U8, name=name, align_bytes=64)
+            nc.vector.tensor_copy(plane[:].bitcast(I32), picked[:].bitcast(I32))
+            for j in range(1, PACK):
+                nc.scalar.dma_start(plane[j:P:32, :].bitcast(I32), picked[8 * j : P : 32, :].bitcast(I32))
+            return plane
+
+        ds_pick = big.tile([P, H], U8, name="ds_pick", align_bytes=64)
+        nc.vector.tensor_copy(ds_pick[:], ds_tab[:].indirect(k1_sb[:]))
+        xs_pick = big.tile([P, S], U8, name="xs_pick", align_bytes=64)
+        nc.vector.tensor_copy(xs_pick[:], xs_tab[:].indirect(offs_sb[:]))
+        xs_final = scale_rows_home(xs_pick, "xs_final")
+        ds_dealt = big.tile([P, H], U8, name="ds_dealt", tag="slot_c", align_bytes=64)
+        nc.vector.tensor_copy(ds_dealt[:].rearrange("p (t m) -> p m t", t=PACK), ds_pick[:].rearrange("p (m t) -> p m t", t=PACK))
+        ds_final = big.tile([P, H], U8, name="ds_final", align_bytes=64)
+        nc.gpsimd.memset(ds_final[:].bitcast(I32), 0)
+        for j in range(PACK):
+            nc.scalar.dma_start(ds_final[j:P:32, :].bitcast(I32), ds_dealt[8 * j : P : 32, :].bitcast(I32))
+
+        dw_pick = big.tile([P, H], U32, name="dw_pick", align_bytes=64)
+        nc.vector.tensor_copy(dw_pick[:], dw_tab[:].bitcast(U32).indirect(k1_sb[:]))
+        xw_pick = big.tile([P, S], U32, name="xw_pick", tag="slot_e", align_bytes=64)
+        nc.vector.tensor_copy(xw_pick[:], xw_tab[:].bitcast(U32).indirect(offs_sb[:]))
+        dw_dealt = big.tile([P, H], U32, name="dw_dealt", tag="slot_h", align_bytes=64)
+        nc.vector.tensor_copy(
+            dw_dealt[:].bitcast(I32).rearrange("p (t m) -> p m t", t=PACK),
+            dw_pick[:].bitcast(I32).rearrange("p (m t) -> p m t", t=PACK),
+        )
+
+        w_raw = big.tile([P, PACK, N], F32, name="w_raw", tag="slot_c", align_bytes=64)
+        nc.sync.dma_start(w_raw[:], w1.rearrange("(p j) m -> p j m", j=PACK))
+
+        hs = []
+        h_planes = big.tile([P, PACK, S], F32, name="h_planes", align_bytes=64)
+        for t in range(PACK):
+            acc = psum.tile([P, S], F32, name="acc", tag="bank")
+            cols = slice(t * P, (t + 1) * P)
+            nc.tensor.matmul_mx(
+                out=acc[:], lhsT=dw_dealt[:, cols].bitcast(FP8X4), lhsT_scale=ds_final[:, cols],
+                rhs=xw_pick[:].bitcast(FP8X4), rhs_scale=xs_final[:], start=True, stop=True,
+            )
+            h = big.tile([P, S], F32, name="h%d" % t, align_bytes=64)
+            if t % 2 == 0:
+                nc.scalar.activation(h[:], acc[:], ACT.Copy, scale=gabs[:, t : t + 1])
+            else:
+                nc.vector.tensor_scalar(h[:], acc[:], gabs[:, t : t + 1], None, ALU.mult)
+            nc.sync.dma_start(h_planes[:, t, :], h[:])
+            hs.append(h)
+
+        w_bf = big.tile([P, N, PACK], BF16, name="w_bf", tag="slot_f", align_bytes=64)
+        nc.vector.tensor_tensor(
+            w_bf[:].rearrange("p (c i) j -> p c j i", i=LINE),
+            w_raw[:].rearrange("p j (c i) -> p c j i", i=LINE),
+            sign[:].unsqueeze(1).unsqueeze(3).to_broadcast([P, N // LINE, PACK, LINE]),
+            ALU.mult,
+        )
+        w_codes = big.tile([P, N], U32, name="w_codes", align_bytes=64)
+        w_scales = big.tile([P, N], U8, name="w_scales", align_bytes=64)
+        nc.vector.quantize_mx(out=w_codes[:].bitcast(FP8X4), scales=w_scales[:], in_=w_bf[:].rearrange("p m j -> p (m j)"))
+
+        pages = []
+        for a, tag in enumerate(("slot_d", "slot_e", "slot_h", "slot_f")):
+            page = big.tile([P, U], F32, name="page%d" % a, tag=tag, align_bytes=64)
+            nc.sync.dma_start(page[:], mem[a * P : (a + 1) * P, :])
+            pages.append(page)
+
+        def middle(half):
+            lst = slice(half * HALF // 16, (half + 1) * HALF // 16)
+            tok = slice(half * HALF, (half + 1) * HALF)
+            mid = big.tile([P, 2, PACK, HALF], F32, name="mid%d" % half, tag="slot_c", align_bytes=64)
+            diff = mid[:, 1]
+            larger = mid[:, 0]
+
+            def take_larger(t):
+                at2 = big.tile([P, HALF], F32, name="at2_%d" % t)
+                at3 = big.tile([P, HALF], F32, name="at3_%d" % t)
+                nc.scalar.activation(at2[:], hs[t][:].indirect(n2_sb[:, lst]), ACT.Copy)
+                nc.scalar.activation(at3[:], hs[t][:].indirect(n3_sb[:, lst]), ACT.Copy)
+                nc.vector.tensor_tensor(larger[:, t, :], at2[:], at3[:], ALU.max)
+
+            take_larger(0)
+            for t in range(PACK):
+                if t + 1 < PACK:
+                    take_larger(t + 1)
+                nc.vector.tensor_tensor(diff[:, t, :], hs[t][:].indirect(n1_sb[:, lst]), larger[:, t, :], ALU.subtract)
+            z_bf = big.tile([P, HALF, PACK], BF16, name="z_bf%d" % half, align_bytes=64)
+            nc.vector.tensor_tensor(
+                z_bf[:].rearrange("p (c i) t -> p c t i", i=LINE),
+                diff.rearrange("p t (c i) -> p c t i", i=LINE),
+                h_planes[:, :, tok].rearrange("p t (c i) -> p c t i", i=LINE),
+                ALU.add,
+            )
+            z_codes = big.tile([P, HALF], U32, name="z_codes%d" % half, align_bytes=64)
+            z_scales = big.tile([P, HALF], U8, name="z_scales%d" % half, align_bytes=64)
+            nc.vector.quantize_mx(out=z_codes[:].bitcast(FP8X4), scales=z_scales[:], in_=z_bf[:].rearrange("p c t -> p (c t)"))
+            return z_codes, z_scales
+
+        def put(half, a, z, on_scalar):
+            lst = slice(half * HALF // 16, (half + 1) * HALF // 16)
+            cols = slice(a * P, (a + 1) * P)
+            acc = psum.tile([P, HALF], F32, name="acc2", tag="bank")
+            nc.tensor.matmul_mx(
+                out=acc[:], lhsT=w_codes[:, cols].bitcast(FP8X4), lhsT_scale=w_scales[:, cols],
+                rhs=z[0][:].bitcast(FP8X4), rhs_scale=z[1][:], start=True, stop=True,
+            )
+            h2 = work.tile([P, HALF], F32, name="h2", bufs=8)
+            if on_scalar:
+                nc.scalar.copy(h2[:], acc[:])
+                nc.scalar.activation(pages[a][:].indirect(n4_sb[:, lst]), h2[:], ACT.Copy)
+            else:
+                nc.vector.tensor_copy(h2[:], acc[:])
+                nc.vector.tensor_copy(pages[a][:].indirect(n4_sb[:, lst]), h2[:])
+
+        z0 = middle(0)
+        z1 = middle(1)
+        for a in range(PACK):
+            put(0, a, z0, True)
+        for a in range(PACK):
+            put(1, a, z1, a == 3)
+            nc.sync.dma_start(out[a * P : (a + 1) * P, :], pages[a][:])

@@ -26,7 +26,6 @@ def tile_picked_pqlaytrimpage_none_p_kernel(tc, x_words, x_scales, d_words, d_sc
     with ExitStack() as ctx:
         keep = ctx.enter_context(tc.tile_pool(name="keep", bufs=1))
         big = ctx.enter_context(tc.tile_pool(name="big", bufs=1))
-        work = ctx.enter_context(tc.tile_pool(name="work", bufs=4))
         psum = ctx.enter_context(tc.psum_pool(name="psum", bufs=8))
 
         def load_list(src, name):
@@ -35,23 +34,32 @@ def tile_picked_pqlaytrimpage_none_p_kernel(tc, x_words, x_scales, d_words, d_sc
             return t
 
         ds_tab = big.tile([P, G], U8, name="ds_tab", align_bytes=64)
-        xs_tab = big.tile([P, T], U8, name="xs_tab", align_bytes=64)
+        xs_tab = big.tile([P, T], U8, name="xs_tab", tag="slot_b", align_bytes=64)
         nc.vector.memset(ds_tab[:].bitcast(I32), 0)
         nc.gpsimd.memset(xs_tab[:].bitcast(I32), 0)
-        nc.sync.dma_start(ds_tab[0:P:8, :].bitcast(I32), d_scales[0].bitcast(I32))
-        nc.sync.dma_start(xs_tab[0:P:8, :].bitcast(I32), x_scales[0].bitcast(I32))
         k1_sb = load_list(k1, "k1_sb")
+        nc.sync.dma_start(ds_tab[0:P:8, :].bitcast(I32), d_scales[0].bitcast(I32))
         offs_sb = load_list(offs, "offs_sb")
-        n2_sb = load_list(n2, "n2_sb")
+        for q in range(4):
+            queue = nc.sync if q < 2 else nc.scalar
+            queue.dma_start(xs_tab[32 * q : 32 * q + 4, :].bitcast(I32), x_scales[0, 4 * q : 4 * q + 4, :].bitcast(I32))
         dw_tab = big.tile([P, G], I32, name="dw_tab", align_bytes=64)
         nc.sync.dma_start(dw_tab[:], d_words[0].rearrange("p n t -> p (n t)").bitcast(I32))
-        n3_sb = load_list(n3, "n3_sb")
-        n1_sb = load_list(n1, "n1_sb")
-        n4_sb = load_list(n4, "n4_sb")
         xw_tab = big.tile([P, T], I32, name="xw_tab", tag="slot_d", align_bytes=64)
         nc.sync.dma_start(xw_tab[:], x_words[0].rearrange("p n t -> p (n t)").bitcast(I32))
         gain = keep.tile([P, PACK], F32, name="gain")
-        nc.gpsimd.dma_start(gain[:], gn.rearrange("(p t) o -> p (t o)", t=PACK))
+        nc.sync.dma_start(gain[:], gn.rearrange("(p t) o -> p (t o)", t=PACK))
+
+        def load_w(half, tag):
+            w_raw = big.tile([P, PACK, HALF], F32, name="w_raw%d" % half, tag=tag, align_bytes=64)
+            nc.sync.dma_start(w_raw[:], w1[:, half * HALF : (half + 1) * HALF].rearrange("(p j) m -> p j m", j=PACK))
+            return w_raw
+
+        w_raws = [load_w(0, "w_first")]
+        n2_sb = load_list(n2, "n2_sb")
+        n3_sb = load_list(n3, "n3_sb")
+        n1_sb = load_list(n1, "n1_sb")
+        n4_sb = load_list(n4, "n4_sb")
 
         gabs = keep.tile([P, PACK], F32, name="gabs")
         nc.scalar.activation(gabs[:], gain[:], ACT.Abs, scale=0.0625)
@@ -60,76 +68,83 @@ def tile_picked_pqlaytrimpage_none_p_kernel(tc, x_words, x_scales, d_words, d_sc
         sign = keep.tile([P, PACK], F32, name="sign")
         nc.gpsimd.tensor_scalar(sign[:], nonneg[:], 1.0, -1.0, ALU.mult, ALU.add)
 
-        def scale_rows_home(picked, name):
-            plane = big.tile([P, S], U8, name=name, align_bytes=64)
-            nc.vector.tensor_copy(plane[:].bitcast(I32), picked[:].bitcast(I32))
-            for j in range(1, PACK):
-                nc.scalar.dma_start(plane[j:P:32, :].bitcast(I32), picked[8 * j : P : 32, :].bitcast(I32))
-            return plane
-
         ds_pick = big.tile([P, H], U8, name="ds_pick", align_bytes=64)
         nc.vector.tensor_copy(ds_pick[:], ds_tab[:].indirect(k1_sb[:]))
         xs_pick = big.tile([P, S], U8, name="xs_pick", align_bytes=64)
         nc.vector.tensor_copy(xs_pick[:], xs_tab[:].indirect(offs_sb[:]))
-        xs_final = scale_rows_home(xs_pick, "xs_final")
-        ds_dealt = big.tile([P, H], U8, name="ds_dealt", tag="slot_c", align_bytes=64)
+        ds_dealt = big.tile([P, H], U8, name="ds_dealt", align_bytes=64)
         nc.vector.tensor_copy(ds_dealt[:].rearrange("p (t m) -> p m t", t=PACK), ds_pick[:].rearrange("p (m t) -> p m t", t=PACK))
         ds_final = big.tile([P, H], U8, name="ds_final", align_bytes=64)
         nc.gpsimd.memset(ds_final[:].bitcast(I32), 0)
-        for j in range(PACK):
-            nc.scalar.dma_start(ds_final[j:P:32, :].bitcast(I32), ds_dealt[8 * j : P : 32, :].bitcast(I32))
+        for q in range(4):
+            nc.scalar.dma_start(ds_final[32 * q : 32 * q + 4, :].bitcast(I32), ds_dealt[32 * q : 32 * q + 32 : 8, :].bitcast(I32))
 
         dw_pick = big.tile([P, H], U32, name="dw_pick", align_bytes=64)
         nc.vector.tensor_copy(dw_pick[:], dw_tab[:].bitcast(U32).indirect(k1_sb[:]))
-        xw_pick = big.tile([P, S], U32, name="xw_pick", tag="slot_e", align_bytes=64)
-        nc.vector.tensor_copy(xw_pick[:], xw_tab[:].bitcast(U32).indirect(offs_sb[:]))
         dw_dealt = big.tile([P, H], U32, name="dw_dealt", tag="slot_h", align_bytes=64)
         nc.vector.tensor_copy(
             dw_dealt[:].bitcast(I32).rearrange("p (t m) -> p m t", t=PACK),
             dw_pick[:].bitcast(I32).rearrange("p (m t) -> p m t", t=PACK),
         )
 
-        w_raw = big.tile([P, PACK, N], F32, name="w_raw", tag="slot_c", align_bytes=64)
-        nc.sync.dma_start(w_raw[:], w1.rearrange("(p j) m -> p j m", j=PACK))
+        xw_picks = []
+        for half in range(2):
+            xw_pick = big.tile([P, HALF], U32, name="xw_pick%d" % half, tag="slot_e%d" % half, align_bytes=64)
+            nc.vector.tensor_copy(xw_pick[:], xw_tab[:].bitcast(U32).indirect(offs_sb[:, half * HALF // 16 : (half + 1) * HALF // 16]))
+            xw_picks.append(xw_pick)
+
+        w_raws.append(load_w(1, "slot_b"))
+
+        def quantise_w(half):
+            w_bf = big.tile([P, HALF, PACK], BF16, name="w_bf%d" % half, tag="w_bf%d" % half, align_bytes=64)
+            nc.vector.tensor_tensor(
+                w_bf[:].rearrange("p (c i) j -> p c j i", i=LINE),
+                w_raws[half][:].rearrange("p j (c i) -> p c j i", i=LINE),
+                sign[:].unsqueeze(1).unsqueeze(3).to_broadcast([P, HALF // LINE, PACK, LINE]),
+                ALU.mult,
+            )
+            codes = big.tile([P, HALF], U32, name="w_codes%d" % half, align_bytes=64)
+            scales = big.tile([P, HALF], U8, name="w_scales%d" % half, align_bytes=64)
+            nc.vector.quantize_mx(out=codes[:].bitcast(FP8X4), scales=scales[:], in_=w_bf[:].rearrange("p m j -> p (m j)"))
+            return codes, scales
+
+        w_mx = [quantise_w(0)]
 
         hs = []
         h_planes = big.tile([P, PACK, S], F32, name="h_planes", align_bytes=64)
+        accs = [psum.tile([P, S], F32, name="acc%d" % t, tag="bank") for t in range(PACK)]
+        for pair in range(0, PACK, 2):
+            for half in range(2):
+                for t in (pair, pair + 1):
+                    cols = slice(t * P, (t + 1) * P)
+                    tok = slice(half * HALF, (half + 1) * HALF)
+                    nc.tensor.matmul_mx(
+                        out=accs[t][:, tok], lhsT=dw_dealt[:, cols].bitcast(FP8X4), lhsT_scale=ds_final[:, cols],
+                        rhs=xw_picks[half][:].bitcast(FP8X4), rhs_scale=xs_pick[:, tok], start=True, stop=True,
+                    )
         for t in range(PACK):
-            acc = psum.tile([P, S], F32, name="acc", tag="bank")
-            cols = slice(t * P, (t + 1) * P)
-            nc.tensor.matmul_mx(
-                out=acc[:], lhsT=dw_dealt[:, cols].bitcast(FP8X4), lhsT_scale=ds_final[:, cols],
-                rhs=xw_pick[:].bitcast(FP8X4), rhs_scale=xs_final[:], start=True, stop=True,
-            )
+            acc = accs[t]
             h = big.tile([P, S], F32, name="h%d" % t, align_bytes=64)
-            if t % 2 == 0:
+            if t == 0:
                 nc.scalar.activation(h[:], acc[:], ACT.Copy, scale=gabs[:, t : t + 1])
             else:
                 nc.vector.tensor_scalar(h[:], acc[:], gabs[:, t : t + 1], None, ALU.mult)
             nc.sync.dma_start(h_planes[:, t, :], h[:])
             hs.append(h)
 
-        w_bf = big.tile([P, N, PACK], BF16, name="w_bf", tag="slot_f", align_bytes=64)
-        nc.vector.tensor_tensor(
-            w_bf[:].rearrange("p (c i) j -> p c j i", i=LINE),
-            w_raw[:].rearrange("p j (c i) -> p c j i", i=LINE),
-            sign[:].unsqueeze(1).unsqueeze(3).to_broadcast([P, N // LINE, PACK, LINE]),
-            ALU.mult,
-        )
-        w_codes = big.tile([P, N], U32, name="w_codes", align_bytes=64)
-        w_scales = big.tile([P, N], U8, name="w_scales", align_bytes=64)
-        nc.vector.quantize_mx(out=w_codes[:].bitcast(FP8X4), scales=w_scales[:], in_=w_bf[:].rearrange("p m j -> p (m j)"))
+        w_mx.append(quantise_w(1))
 
-        pages = []
-        for a, tag in enumerate(("slot_d", "slot_e", "slot_h", "slot_f")):
+        def load_page(a, tag):
             page = big.tile([P, U], F32, name="page%d" % a, tag=tag, align_bytes=64)
             nc.sync.dma_start(page[:], mem[a * P : (a + 1) * P, :])
-            pages.append(page)
+            return page
+
+        pages = {0: load_page(0, "slot_d"), 3: load_page(3, "w_bf0"), 1: load_page(1, "w_bf1")}
 
         def middle(half):
             lst = slice(half * HALF // 16, (half + 1) * HALF // 16)
             tok = slice(half * HALF, (half + 1) * HALF)
-            mid = big.tile([P, 2, PACK, HALF], F32, name="mid%d" % half, tag="slot_c", align_bytes=64)
+            mid = big.tile([P, 2, PACK, HALF], F32, name="mid%d" % half, tag="slot_b", align_bytes=64)
             diff = mid[:, 1]
             larger = mid[:, 0]
 
@@ -145,7 +160,7 @@ def tile_picked_pqlaytrimpage_none_p_kernel(tc, x_words, x_scales, d_words, d_sc
                 if t + 1 < PACK:
                     take_larger(t + 1)
                 nc.vector.tensor_tensor(diff[:, t, :], hs[t][:].indirect(n1_sb[:, lst]), larger[:, t, :], ALU.subtract)
-            z_bf = big.tile([P, HALF, PACK], BF16, name="z_bf%d" % half, align_bytes=64)
+            z_bf = big.tile([P, HALF, PACK], BF16, name="z_bf%d" % half, tag="z_bf%d" % half, align_bytes=64)
             nc.vector.tensor_tensor(
                 z_bf[:].rearrange("p (c i) t -> p c t i", i=LINE),
                 diff.rearrange("p t (c i) -> p c t i", i=LINE),
@@ -157,26 +172,39 @@ def tile_picked_pqlaytrimpage_none_p_kernel(tc, x_words, x_scales, d_words, d_sc
             nc.vector.quantize_mx(out=z_codes[:].bitcast(FP8X4), scales=z_scales[:], in_=z_bf[:].rearrange("p c t -> p (c t)"))
             return z_codes, z_scales
 
-        def put(half, a, z, on_scalar):
-            lst = slice(half * HALF // 16, (half + 1) * HALF // 16)
-            cols = slice(a * P, (a + 1) * P)
-            acc = psum.tile([P, HALF], F32, name="acc2", tag="bank")
-            nc.tensor.matmul_mx(
-                out=acc[:], lhsT=w_codes[:, cols].bitcast(FP8X4), lhsT_scale=w_scales[:, cols],
-                rhs=z[0][:].bitcast(FP8X4), rhs_scale=z[1][:], start=True, stop=True,
-            )
-            h2 = work.tile([P, HALF], F32, name="h2", bufs=8)
+        def product(z, blocks, on_scalar, tag):
+            acc = psum.tile([P, len(blocks), HALF], F32, name="acc2", tag="bank")
+            for i, a in enumerate(blocks):
+                codes, scales = w_mx[a // 2]
+                cols = slice(a % 2 * P, (a % 2 + 1) * P)
+                nc.tensor.matmul_mx(
+                    out=acc[:, i, :], lhsT=codes[:, cols].bitcast(FP8X4), lhsT_scale=scales[:, cols],
+                    rhs=z[0][:].bitcast(FP8X4), rhs_scale=z[1][:], start=True, stop=True,
+                )
+            h2 = big.tile([P, len(blocks), HALF], F32, name="h2", tag=tag, align_bytes=64)
             if on_scalar:
                 nc.scalar.copy(h2[:], acc[:])
-                nc.scalar.activation(pages[a][:].indirect(n4_sb[:, lst]), h2[:], ACT.Copy)
             else:
                 nc.vector.tensor_copy(h2[:], acc[:])
-                nc.vector.tensor_copy(pages[a][:].indirect(n4_sb[:, lst]), h2[:])
+            return h2
+
+        def put(half, a, values, on_scalar):
+            window = pages[a][:].indirect(n4_sb[:, half * HALF // 16 : (half + 1) * HALF // 16])
+            if on_scalar:
+                nc.scalar.activation(window, values, ACT.Copy)
+            else:
+                nc.vector.tensor_copy(window, values)
 
         z0 = middle(0)
+        pages[2] = load_page(2, "z_bf0")
         z1 = middle(1)
-        for a in range(PACK):
-            put(0, a, z0, True)
-        for a in range(PACK):
-            put(1, a, z1, a == 3)
-            nc.sync.dma_start(out[a * P : (a + 1) * P, :], pages[a][:])
+        h2 = product(z0, (0, 1), True, "h2_first")
+        put(0, 0, h2[:, 0, :], True)
+        put(0, 1, h2[:, 1, :], True)
+        put(0, 2, product(z0, (2,), True, "h2_third")[:, 0, :], True)
+        put(0, 3, product(z0, (3,), False, "z_bf1")[:, 0, :], False)
+        for a in (3, 1, 0, 2):
+            on_scalar = a in (1, 2)
+            put(1, a, product(z1, (a,), on_scalar, "h2_last%d" % a)[:, 0, :], on_scalar)
+            queue = nc.scalar if on_scalar else nc.sync
+            queue.dma_start(out[a * P : (a + 1) * P, :], pages[a][:])

@@ -188,8 +188,9 @@ def tile_picked_pqlaytrimpage_none_p_kernel(tc, x_words, x_scales, d_words, d_sc
                 nc.vector.tensor_copy(h2[:], acc[:])
             return h2
 
-        def put(half, a, values, on_scalar):
-            window = pages[a][:].indirect(n4_sb[:, half * HALF // 16 : (half + 1) * HALF // 16])
+        def put(first, a, values, on_scalar):
+            count = values.shape[1]
+            window = pages[a][:].indirect(n4_sb[:, first // 16 : (first + count) // 16])
             if on_scalar:
                 nc.scalar.activation(window, values, ACT.Copy)
             else:
@@ -205,6 +206,11 @@ def tile_picked_pqlaytrimpage_none_p_kernel(tc, x_words, x_scales, d_words, d_sc
         put(0, 3, product(z0, (3,), False, "z_bf1")[:, 0, :], False)
         for a in (3, 1, 0, 2):
             on_scalar = a in (1, 2)
-            put(1, a, product(z1, (a,), on_scalar, "h2_last%d" % a)[:, 0, :], on_scalar)
+            h2 = product(z1, (a,), on_scalar, "h2_last%d" % a)
+            if a == 0:
+                put(HALF, a, h2[:, 0, 0 : HALF // 2], True)
+                put(HALF + HALF // 2, a, h2[:, 0, HALF // 2 : HALF], False)
+            else:
+                put(HALF, a, h2[:, 0, :], on_scalar)
             queue = nc.scalar if on_scalar else nc.sync
             queue.dma_start(out[a * P : (a + 1) * P, :], pages[a][:])

from contextlib import ExitStack

import concourse.mybir as mybir

K, T, S, N, G, H, U = 512, 2048, 512, 512, 2048, 512, 1024
FLOPS = 2 * K * H * S + 2 * H * N * S

F32 = mybir.dt.float32
BF16 = mybir.dt.bfloat16
I32 = mybir.dt.int32
U32 = mybir.dt.uint32
U16 = mybir.dt.uint16
U8 = mybir.dt.uint8
FP8X4 = mybir.dt.float8_e4m3fn_x4
ALU = mybir.AluOpType
ACT = mybir.ActivationFunctionType

P = 128
PACK = 4
HALF = S // 2
LINE = 4


def tile_picked_pqlaytrimpage_none_p_kernel(tc, x_words, x_scales, d_words, d_scales, gn, w1, mem, offs, k1, n1, n2, n3, n4, out):
    nc = tc.nc
    with ExitStack() as ctx:
        keep = ctx.enter_context(tc.tile_pool(name="keep", bufs=1))
        big = ctx.enter_context(tc.tile_pool(name="big", bufs=1))
        psum = ctx.enter_context(tc.psum_pool(name="psum", bufs=8))

        def load_list(src, name):
            t = keep.tile([P, S // 16], U16, name=name)
            nc.sync.dma_start(t[:], src)
            return t

        ds_tab = big.tile([P, G], U8, name="ds_tab", align_bytes=64)
        xs_tab = big.tile([P, T], U8, name="xs_tab", tag="slot_b", align_bytes=64)
        nc.vector.memset(ds_tab[:].bitcast(I32), 0)
        nc.gpsimd.memset(xs_tab[:].bitcast(I32), 0)
        k1_sb = load_list(k1, "k1_sb")
        nc.sync.dma_start(ds_tab[0:P:8, :].bitcast(I32), d_scales[0].bitcast(I32))
        offs_sb = load_list(offs, "offs_sb")
        for q in range(4):
            queue = nc.sync if q < 2 else nc.scalar
            queue.dma_start(xs_tab[32 * q : 32 * q + 4, :].bitcast(I32), x_scales[0, 4 * q : 4 * q + 4, :].bitcast(I32))
        dw_tab = big.tile([P, G], I32, name="dw_tab", align_bytes=64)
        nc.sync.dma_start(dw_tab[:], d_words[0].rearrange("p n t -> p (n t)").bitcast(I32))
        xw_tab = big.tile([P, T], I32, name="xw_tab", tag="slot_d", align_bytes=64)
        nc.sync.dma_start(xw_tab[:], x_words[0].rearrange("p n t -> p (n t)").bitcast(I32))
        gain = keep.tile([P, PACK], F32, name="gain")
        nc.sync.dma_start(gain[:], gn.rearrange("(p t) o -> p (t o)", t=PACK))

        def load_w(half, tag):
            w_raw = big.tile([P, PACK, HALF], F32, name="w_raw%d" % half, tag=tag, align_bytes=64)
            nc.sync.dma_start(w_raw[:], w1[:, half * HALF : (half + 1) * HALF].rearrange("(p j) m -> p j m", j=PACK))
            return w_raw

        w_raws = [load_w(0, "w_first")]
        n2_sb = load_list(n2, "n2_sb")
        n3_sb = load_list(n3, "n3_sb")
        n1_sb = load_list(n1, "n1_sb")
        n4_sb = load_list(n4, "n4_sb")

        gabs = keep.tile([P, PACK], F32, name="gabs")
        nc.scalar.activation(gabs[:], gain[:], ACT.Abs, scale=0.0625)
        nonneg = keep.tile([P, PACK], F32, name="nonneg")
        nc.gpsimd.tensor_scalar(nonneg[:], gain[:], 0.0, 2.0, ALU.is_ge, ALU.mult)
        sign = keep.tile([P, PACK], F32, name="sign")
        nc.gpsimd.tensor_scalar(sign[:], nonneg[:], 1.0, -1.0, ALU.mult, ALU.add)

        ds_pick = big.tile([P, H], U8, name="ds_pick", align_bytes=64)
        nc.vector.tensor_copy(ds_pick[:], ds_tab[:].indirect(k1_sb[:]))
        xs_pick = big.tile([P, S], U8, name="xs_pick", align_bytes=64)
        nc.vector.tensor_copy(xs_pick[:], xs_tab[:].indirect(offs_sb[:]))
        ds_dealt = big.tile([P, H], U8, name="ds_dealt", align_bytes=64)
        nc.vector.tensor_copy(ds_dealt[:].rearrange("p (t m) -> p m t", t=PACK), ds_pick[:].rearrange("p (m t) -> p m t", t=PACK))
        ds_final = big.tile([P, H], U8, name="ds_final", align_bytes=64)
        nc.gpsimd.memset(ds_final[:].bitcast(I32), 0)
        for q in range(4):
            nc.scalar.dma_start(ds_final[32 * q : 32 * q + 4, :].bitcast(I32), ds_dealt[32 * q : 32 * q + 32 : 8, :].bitcast(I32))

        dw_pick = big.tile([P, H], U32, name="dw_pick", align_bytes=64)
        nc.vector.tensor_copy(dw_pick[:], dw_tab[:].bitcast(U32).indirect(k1_sb[:]))
        dw_dealt = big.tile([P, H], U32, name="dw_dealt", tag="slot_h", align_bytes=64)
        nc.vector.tensor_copy(
            dw_dealt[:].bitcast(I32).rearrange("p (t m) -> p m t", t=PACK),
            dw_pick[:].bitcast(I32).rearrange("p (m t) -> p m t", t=PACK),
        )

        xw_picks = []
        for half in range(2):
            xw_pick = big.tile([P, HALF], U32, name="xw_pick%d" % half, tag="slot_e%d" % half, align_bytes=64)
            nc.vector.tensor_copy(xw_pick[:], xw_tab[:].bitcast(U32).indirect(offs_sb[:, half * HALF // 16 : (half + 1) * HALF // 16]))
            xw_picks.append(xw_pick)

        w_raws.append(load_w(1, "slot_b"))

        def quantise_w(half):
            w_bf = big.tile([P, HALF, PACK], BF16, name="w_bf%d" % half, tag="w_bf%d" % half, align_bytes=64)
            nc.vector.tensor_tensor(
                w_bf[:].rearrange("p (c i) j -> p c j i", i=LINE),
                w_raws[half][:].rearrange("p j (c i) -> p c j i", i=LINE),
                sign[:].unsqueeze(1).unsqueeze(3).to_broadcast([P, HALF // LINE, PACK, LINE]),
                ALU.mult,
            )
            codes = big.tile([P, HALF], U32, name="w_codes%d" % half, align_bytes=64)
            scales = big.tile([P, HALF], U8, name="w_scales%d" % half, align_bytes=64)
            nc.vector.quantize_mx(out=codes[:].bitcast(FP8X4), scales=scales[:], in_=w_bf[:].rearrange("p m j -> p (m j)"))
            return codes, scales

        w_mx = [quantise_w(0)]

        hs = []
        h_planes = big.tile([P, PACK, S], F32, name="h_planes", align_bytes=64)
        accs = [psum.tile([P, S], F32, name="acc%d" % t, tag="bank") for t in range(PACK)]
        for pair in range(0, PACK, 2):
            for half in range(2):
                for t in (pair, pair + 1):
                    cols = slice(t * P, (t + 1) * P)
                    tok = slice(half * HALF, (half + 1) * HALF)
                    nc.tensor.matmul_mx(
                        out=accs[t][:, tok], lhsT=dw_dealt[:, cols].bitcast(FP8X4), lhsT_scale=ds_final[:, cols],
                        rhs=xw_picks[half][:].bitcast(FP8X4), rhs_scale=xs_pick[:, tok], start=True, stop=True,
                    )
        for t in range(PACK):
            acc = accs[t]
            h = big.tile([P, S], F32, name="h%d" % t, align_bytes=64)
            if t == 0:
                nc.scalar.activation(h[:], acc[:], ACT.Copy, scale=gabs[:, t : t + 1])
            else:
                nc.vector.tensor_scalar(h[:], acc[:], gabs[:, t : t + 1], None, ALU.mult)
            nc.sync.dma_start(h_planes[:, t, :], h[:])
            hs.append(h)

        w_mx.append(quantise_w(1))

        def load_page(a, tag):
            page = big.tile([P, U], F32, name="page%d" % a, tag=tag, align_bytes=64)
            nc.sync.dma_start(page[:], mem[a * P : (a + 1) * P, :])
            return page

        pages = {0: load_page(0, "slot_d"), 3: load_page(3, "w_bf0"), 1: load_page(1, "w_bf1")}

        def middle(half):
            lst = slice(half * HALF // 16, (half + 1) * HALF // 16)
            tok = slice(half * HALF, (half + 1) * HALF)
            mid = big.tile([P, 2, PACK, HALF], F32, name="mid%d" % half, tag="slot_b", align_bytes=64)
            diff = mid[:, 1]
            larger = mid[:, 0]

            def take_larger(t):
                at2 = big.tile([P, HALF], F32, name="at2_%d" % t)
                at3 = big.tile([P, HALF], F32, name="at3_%d" % t)
                nc.scalar.activation(at2[:], hs[t][:].indirect(n2_sb[:, lst]), ACT.Copy)
                nc.scalar.activation(at3[:], hs[t][:].indirect(n3_sb[:, lst]), ACT.Copy)
                nc.vector.tensor_tensor(larger[:, t, :], at2[:], at3[:], ALU.max)

            take_larger(0)
            for t in range(PACK):
                if t + 1 < PACK:
                    take_larger(t + 1)
                nc.vector.tensor_tensor(diff[:, t, :], hs[t][:].indirect(n1_sb[:, lst]), larger[:, t, :], ALU.subtract)
            z_bf = big.tile([P, HALF, PACK], BF16, name="z_bf%d" % half, tag="z_bf%d" % half, align_bytes=64)
            nc.vector.tensor_tensor(
                z_bf[:].rearrange("p (c i) t -> p c t i", i=LINE),
                diff.rearrange("p t (c i) -> p c t i", i=LINE),
                h_planes[:, :, tok].rearrange("p t (c i) -> p c t i", i=LINE),
                ALU.add,
            )
            z_codes = big.tile([P, HALF], U32, name="z_codes%d" % half, align_bytes=64)
            z_scales = big.tile([P, HALF], U8, name="z_scales%d" % half, align_bytes=64)
            nc.vector.quantize_mx(out=z_codes[:].bitcast(FP8X4), scales=z_scales[:], in_=z_bf[:].rearrange("p c t -> p (c t)"))
            return z_codes, z_scales

        def product(z, blocks, on_scalar, tag):
            acc = psum.tile([P, len(blocks), HALF], F32, name="acc2", tag="bank")
            for i, a in enumerate(blocks):
                codes, scales = w_mx[a // 2]
                cols = slice(a % 2 * P, (a % 2 + 1) * P)
                nc.tensor.matmul_mx(
                    out=acc[:, i, :], lhsT=codes[:, cols].bitcast(FP8X4), lhsT_scale=scales[:, cols],
                    rhs=z[0][:].bitcast(FP8X4), rhs_scale=z[1][:], start=True, stop=True,
                )
            h2 = big.tile([P, len(blocks), HALF], F32, name="h2", tag=tag, align_bytes=64)
            if on_scalar:
                nc.scalar.copy(h2[:], acc[:])
            else:
                nc.vector.tensor_copy(h2[:], acc[:])
            return h2

        def put(first, a, values, on_scalar):
            count = values.shape[1]
            window = pages[a][:].indirect(n4_sb[:, first // 16 : (first + count) // 16])
            if on_scalar:
                nc.scalar.activation(window, values, ACT.Copy)
            else:
                nc.vector.tensor_copy(window, values)

        z0 = middle(0)
        pages[2] = load_page(2, "z_bf0")
        z1 = middle(1)
        h2 = product(z0, (0, 1), True, "h2_first")
        put(0, 0, h2[:, 0, :], True)
        put(0, 1, h2[:, 1, :], True)
        put(0, 2, product(z0, (2,), True, "h2_third")[:, 0, :], True)
        put(0, 3, product(z0, (3,), False, "z_bf1")[:, 0, :], False)
        for a in (3, 1, 0, 2):
            on_scalar = a in (1, 2)
            h2 = product(z1, (a,), on_scalar, "h2_last%d" % a)
            if a == 0:
                put(HALF, a, h2[:, 0, 0 : HALF // 2], True)
                put(HALF + HALF // 2, a, h2[:, 0, HALF // 2 : HALF], False)
            else:
                put(HALF, a, h2[:, 0, :], on_scalar)
            queue = nc.scalar if on_scalar else nc.sync
            queue.dma_start(out[a * P : (a + 1) * P, :], pages[a][:])
